import numpy as np
import ml_dtypes


def mxq(x, axis, fmt="e4m3"):
    dtype, down = {"e4m3": (ml_dtypes.float8_e4m3fn, 7), "e5m2": (ml_dtypes.float8_e5m2, 14)}[fmt]
    v = np.moveaxis(np.asarray(x, np.float32).astype(ml_dtypes.bfloat16).astype(np.float64), axis, -1)
    blocks = v.reshape(v.shape[:-1] + (-1, 32))
    amax = np.abs(blocks).max(-1, keepdims=True)
    byte = np.maximum(np.where(amax > 0, np.frexp(amax)[1] - 1 + 127, 0) - down, 1)
    scale = np.exp2(byte - 127.0)
    codes = (blocks / scale).astype(np.float32).astype(dtype).astype(np.float64)
    return np.moveaxis((codes * scale).reshape(v.shape), -1, axis)


WIDE = False


def mx_kscale(k):
    if not WIDE:
        return np.ones(k)
    levels = np.array([30, -30])
    if k % 512:
        return np.exp2(np.random.permutation(np.resize(levels, k // 32))).repeat(32)
    a = np.empty((k // 512, 16))
    for p in range(k // 512):
        a[p, :8] = np.random.permutation(np.resize(levels, 8))
        for g in range(8):
            far = levels[np.abs(levels - a[p, g]) >= 10]
            a[p, g + 8] = far[np.random.randint(len(far))]
    return np.exp2(a.ravel()).repeat(32)


def f64(x):
    return np.asarray(x).astype(np.float64)


def striped(idx):
    return np.tile(np.asarray(idx).reshape(-1, 16).T, (8, 1)).astype(np.uint16)


def unstriped(offs):
    return offs[:16].T.reshape(-1).astype(np.int64)


E2M1 = np.array([0.0, 0.5, 1.0, 1.5, 2.0, 3.0, 4.0, 6.0, -0.0, -0.5, -1.0, -1.5, -2.0, -3.0, -4.0, -6.0])


def pack_weight(w, fmt):
    k, n = w.shape
    w = f64(np.asarray(w, np.float32).astype(ml_dtypes.bfloat16)).reshape(k // 32, 32, n)
    amax = np.abs(w).max(1)
    if fmt == "e4m3":
        byte = np.frexp(amax)[1] - 1 + 127 - 7
    else:
        mant, ex = np.frexp(amax / 6.0)
        byte = np.where(mant > 0.5, ex, ex - 1) + 127
    byte = np.clip(np.where(amax > 0, byte, 1), 1, 254)
    scaled = (w * np.exp2(127.0 - byte)[:, None, :]).reshape(k, n).astype(np.float32)
    by_word = np.ascontiguousarray(scaled.reshape(k // 512, 128, 4, n).transpose(0, 1, 3, 2))
    if fmt == "e4m3":
        words = by_word.astype(ml_dtypes.float8_e4m3fn).view(np.uint8)
    else:
        c = by_word.astype(ml_dtypes.float4_e2m1fn).view(np.uint8) & 0xF
        words = (c[..., 0::2] | (c[..., 1::2] << 4)).reshape(k // 512, 128, 2 * n)
    return np.ascontiguousarray(words), np.ascontiguousarray(byte.astype(np.uint8).reshape(k // 512, 16, n))


def unpack_weight(words, scales, fmt):
    g, _, n = scales.shape
    words = np.ascontiguousarray(words).reshape(g, 128, n, -1)
    if fmt == "e4m3":
        vals = words.view(ml_dtypes.float8_e4m3fn).astype(np.float64)
    else:
        nib = np.empty((g, 128, n, 4), np.uint8)
        nib[..., 0::2] = words & 0xF
        nib[..., 1::2] = words >> 4
        vals = E2M1[nib]
    vals = vals * np.repeat(np.exp2(scales.astype(np.float64) - 127.0), 8, axis=1)[..., None]
    return vals.transpose(0, 1, 3, 2).reshape(g * 512, n)


def bf(x):
    return np.asarray(x, np.float32).astype(ml_dtypes.bfloat16)


def planes(Y):
    r, m = Y.shape
    b = f64(bf(Y)).reshape(r // 32, 32, m)
    amax = np.abs(b).max(1)
    byte = np.clip(np.where(amax > 0, np.frexp(amax)[1] - 1 + 127 - 7, 1), 1, 254)
    codes = (b * np.exp2(127.0 - byte)[:, None, :]).reshape(r, m).astype(np.float32).astype(ml_dtypes.float8_e4m3fn).view(np.uint8)
    words = codes.reshape(r // 512, 128, 4, m).transpose(0, 1, 3, 2)
    return np.ascontiguousarray(words), np.ascontiguousarray(byte.astype(np.uint8).reshape(r // 512, 16, m))


K, T, J, R, O, N = 512, 512, 256, 512, 128, 512


def setup_inputs():
    n = np.random.standard_normal
    idx = np.random.permutation(T)[:J]
    idx2 = np.random.permutation(T)[:J]
    idx3 = np.random.permutation(J)[:O]
    idx4 = np.random.permutation(J)[:O]
    fk = mx_kscale(K)
    fr = mx_kscale(R)
    wp = pack_weight(n((K, R)) * 1 / np.sqrt(K) * fk[:, None] * fr, "e4m3")
    wbp = pack_weight(n((R, N)) * 1 / np.sqrt(R) / fr[:, None], "e2m1")
    return {
        "xf": (n((K, T))).astype(np.float32),
        "fk": (np.random.uniform(0.5, 2.0, (K, 1)) / fk[:, None]).astype(np.float32),
        "w_words": wp[0],
        "w_scales": wp[1],
        "wb_words": wbp[0],
        "wb_scales": wbp[1],
        "rs": (n((N, O))).astype(np.float32),
        "offs": striped(idx),
        "offs2": striped(idx2),
        "offs3": striped(idx3),
        "offs4": striped(idx4),
    }


def reference(xf, fk, w_words, w_scales, wb_words, wb_scales, rs, offs, offs2, offs3, offs4):
    idx = unstriped(offs)
    idx2 = unstriped(offs2)
    idx3 = unstriped(offs3)
    idx4 = unstriped(offs4)
    wu = unpack_weight(w_words, w_scales, "e4m3")
    wbu = unpack_weight(wb_words, wb_scales, "e2m1")
    u = np.maximum(f64(xf)[:, idx], f64(xf)[:, idx2]) * f64(fk)
    uq = mxq(u, 0, "e4m3")
    a = wu.T @ uq
    hid = np.abs(a[:, idx3] - 0.5 * a[:, idx4])
    hidq = mxq(hid, 0, "e5m2")
    p = wbu.T @ hidq
    p1 = np.pad(p, ((0, 0), (1, 0)))[:, :O]
    y = p - 0.7 * p1 + 0.5 * f64(rs)
    words, scales = planes(y)
    return y, words, scales

@@ -1,0 +1,195 @@
+from contextlib import ExitStack
+
+import concourse.mybir as mybir
+
+K, T, J, R, O, N = 512, 512, 256, 512, 128, 512
+FLOPS = 2 * K * R * J + 2 * R * N * O
+
+F32 = mybir.dt.float32
+BF16 = mybir.dt.bfloat16
+I32 = mybir.dt.int32
+U32 = mybir.dt.uint32
+U16 = mybir.dt.uint16
+U8 = mybir.dt.uint8
+E4M3 = mybir.dt.float8_e4m3fn_x4
+E5M2 = mybir.dt.float8_e5m2_x4
+E2M1 = mybir.dt.float4_e2m1fn_x4
+ALU = mybir.AluOpType
+ACT = mybir.ActivationFunctionType
+
+P = 128
+PACK = 4
+RUN = 4
+
+
+def woven(cols):
+    return cols.rearrange("p (c i t) -> p c t i", i=RUN, t=PACK)
+
+
+def by_rows(rows):
+    return rows.rearrange("p t (c i) -> p c t i", i=RUN)
+
+
+def load_scale_rows(queue, tile, scales):
+    for q in range(4):
+        rows = scales[0, 4 * q : 4 * q + 4, :].bitcast(I32)
+        queue.dma_start(out=tile[32 * q : 32 * (q + 1), :].bitcast(I32), in_=rows.unsqueeze(0).broadcast_to([8, 4, rows.shape[1]]))
+
+
+def deal(nc, dealt, raw):
+    nc.vector.tensor_copy(out=dealt.rearrange("p (t m) -> p t m", t=PACK), in_=raw.rearrange("p (m t) -> p t m", t=PACK))
+
+
+def tile_list_looks_largerpicks_farther_lagged_pl_kernel(
+    tc, xf, fk, w_words, w_scales, wb_words, wb_scales, rs, offs, offs2, offs3, offs4, out_0, out_1, out_2
+):
+    nc = tc.nc
+    with ExitStack() as ctx:
+        sb = ctx.enter_context(tc.tile_pool(name="sb", bufs=1))
+        ps = ctx.enter_context(tc.psum_pool(name="ps", bufs=1))
+
+        list1 = sb.tile([P, J // 16], U16, name="list1")
+        list2 = sb.tile([P, J // 16], U16, name="list2")
+        list3 = sb.tile([P, O // 16], U16, name="list3")
+        list4 = sb.tile([P, O // 16], U16, name="list4")
+        x = [sb.tile([P, T], F32, name="x%d" % t) for t in range(PACK)]
+        factor = sb.tile([P, PACK], F32, name="factor")
+        w_raw = sb.tile([P, R], U32, name="w_raw")
+        ws_raw = sb.tile([P, R], U8, name="ws_raw")
+        wb_raw = sb.tile([P, 2 * N], U8, name="wb_raw")
+        wbs_raw = sb.tile([P, N], U8, name="wbs_raw")
+        resid = sb.tile([P, PACK, O], F32, name="resid")
+
+
+        load_scale_rows(nc.gpsimd, wbs_raw, wb_scales)
+        x_rows = xf.rearrange("(p t) c -> p t c", t=PACK)
+        nc.sync.dma_start(out=x[0][:], in_=x_rows[:, 0, :])
+        nc.sync.dma_start(list2[:], offs2)
+        nc.sync.dma_start(list1[:], offs)
+        for t in range(1, PACK):
+            nc.sync.dma_start(out=x[t][:], in_=x_rows[:, t, :])
+        load_scale_rows(nc.sync, ws_raw, w_scales)
+        nc.sync.dma_start(out=factor[:], in_=fk.rearrange("(p t) o -> p (t o)", t=PACK))
+        nc.sync.dma_start(out=w_raw[:].bitcast(I32), in_=w_words[0].rearrange("p c t -> p (c t)").bitcast(I32))
+        nc.sync.dma_start(out=wb_raw[:].bitcast(I32), in_=wb_words[0].bitcast(I32))
+        nc.sync.dma_start(list4[:], offs4)
+        nc.sync.dma_start(list3[:], offs3)
+        nc.sync.dma_start(out=resid[:], in_=rs.rearrange("(p t) o -> p t o", t=PACK))
+
+        w_plane = sb.tile([P, R], U8, name="w_plane", align_bytes=64)
+        deal(nc, w_plane[:], ws_raw[:])
+        last = PACK - 1
+        hj = J // 2
+        first = sb.tile([P, PACK, J], F32, name="first")
+        second = sb.tile([P, PACK, J], F32, name="second")
+        larger = [sb.tile([P, PACK, hj], F32, name="larger%d" % h) for h in range(2)]
+        for t in range(last):
+            nc.scalar.activation(second[:, t, :], x[t][:].indirect(list2[:]), ACT.Copy)
+            nc.vector.tensor_copy(first[:, t, :], x[t][:].indirect(list1[:]))
+        for h in range(2):
+            slots = slice(h * hj, (h + 1) * hj)
+            entries = slice(h * hj // 16, (h + 1) * hj // 16)
+            nc.scalar.activation(second[:, last, slots], x[last][:].indirect(list2[:, entries]), ACT.Copy)
+            nc.scalar.activation(first[:, last, slots], x[last][:].indirect(list1[:, entries]), ACT.Copy)
+        for planes in (slice(0, last), slice(last, PACK)):
+            for h in range(2):
+                slots = slice(h * hj, (h + 1) * hj)
+                nc.vector.tensor_tensor(larger[h][:, planes, :], first[:, planes, slots], second[:, planes, slots], ALU.max)
+
+        u_bf = sb.tile([P, PACK * J], BF16, name="u_bf", tag="shared_a", align_bytes=64)
+        u_codes = sb.tile([P, J], U32, name="u_codes", align_bytes=64)
+        u_plane = sb.tile([P, J], U8, name="u_plane", align_bytes=64)
+        for h in range(2):
+            nc.vector.tensor_tensor(
+                woven(u_bf[:, h * PACK * hj : (h + 1) * PACK * hj]),
+                by_rows(larger[h][:]),
+                factor[:].unsqueeze(1).unsqueeze(3).to_broadcast([P, hj // RUN, PACK, RUN]),
+                ALU.mult,
+            )
+        for h in range(2):
+            slots = slice(h * hj, (h + 1) * hj)
+            nc.vector.quantize_mx(
+                out=u_codes[:, slots].bitcast(E4M3), scales=u_plane[:, slots], in_=u_bf[:, h * PACK * hj : (h + 1) * PACK * hj]
+            )
+
+        w_codes = [sb.tile([P, P], U32, name="w_codes%d" % t, align_bytes=64) for t in range(PACK)]
+        for t in range(PACK):
+            nc.vector.tensor_copy(w_codes[t][:], w_raw[:].rearrange("p (m t) -> p t m", t=PACK)[:, t, :])
+
+        a_ps = [ps.tile([P, J], F32, name="a_ps%d" % t) for t in range(PACK)]
+        for t in range(PACK):
+            for h in range(2):
+                slots = slice(h * hj, (h + 1) * hj)
+                nc.tensor.matmul_mx(
+                    out=a_ps[t][:, slots],
+                    lhsT=w_codes[t][:].bitcast(E4M3),
+                    lhsT_scale=w_plane[:, t * P : (t + 1) * P],
+                    rhs=u_codes[:, slots].bitcast(E4M3),
+                    rhs_scale=u_plane[:, slots],
+                    start=True,
+                    stop=True,
+                )
+
+        wb_dealt = sb.tile([P, 3 * N], U8, name="wb_dealt", tag="shared_a", align_bytes=64)
+        wb_codes = wb_dealt[:, 0 : 2 * N]
+        wb_plane = wb_dealt[:, 2 * N : 3 * N]
+        deal(nc, wb_codes.bitcast(U16), wb_raw[:].bitcast(U16))
+        deal(nc, wb_plane, wbs_raw[:])
+
+        a = [sb.tile([P, J], F32, name="a%d" % t) for t in range(PACK)]
+        half = sb.tile([P, PACK, O], F32, name="half")
+        whole = sb.tile([P, O], F32, name="whole")
+        diff = sb.tile([P, PACK, O], F32, name="diff")
+        nc.scalar.copy(a[0][:], a_ps[0][:])
+        for t in range(1, PACK):
+            nc.vector.tensor_copy(a[t][:], a_ps[t][:])
+        for t in range(PACK):
+            nc.scalar.activation(half[:, t, :], a[t][:].indirect(list4[:]), ACT.Copy, scale=-0.5)
+        nc.scalar.activation(whole[:], a[last][:].indirect(list3[:]), ACT.Copy)
+        for t in range(last):
+            nc.vector.tensor_tensor(diff[:, t, :], a[t][:].indirect(list3[:]), half[:, t, :], ALU.add)
+        nc.vector.tensor_tensor(diff[:, last, :], whole[:], half[:, last, :], ALU.add)
+
+        hid_bf = sb.tile([P, PACK * O], BF16, name="hid_bf", align_bytes=64)
+        ho = O // 2
+        nc.scalar.activation(woven(hid_bf[:, 0 : PACK * ho]), by_rows(diff[:, :, 0:ho]), ACT.Abs)
+        upper = diff[:, :, ho:O].rearrange("p t c -> p c t")
+        nc.vector.scalar_tensor_tensor(
+            hid_bf[:, PACK * ho : PACK * O].rearrange("p (c t) -> p c t", t=PACK), upper, -1.0, upper, ALU.mult, ALU.max
+        )
+        hid_codes = sb.tile([P, O], U32, name="hid_codes", align_bytes=64)
+        hid_plane = sb.tile([P, O], U8, name="hid_plane", align_bytes=64)
+        nc.vector.quantize_mx(out=hid_codes[:].bitcast(E5M2), scales=hid_plane[:], in_=hid_bf[:])
+
+        p_ps = [ps.tile([P, 2, O], F32, name="p_ps%d" % h) for h in range(2)]
+        y = sb.tile([P, PACK, O], F32, name="y")
+        out_rows = out_0.rearrange("(p t) o -> p t o", t=PACK)
+        for t in range(PACK):
+            nc.tensor.matmul_mx(
+                out=p_ps[t // 2][:, t % 2, :],
+                lhsT=wb_codes[:, 2 * t * P : 2 * (t + 1) * P].bitcast(E2M1),
+                lhsT_scale=wb_plane[:, t * P : (t + 1) * P],
+                rhs=hid_codes[:].bitcast(E5M2),
+                rhs_scale=hid_plane[:],
+                start=True,
+                stop=True,
+            )
+        for h in range(2):
+            rows = slice(2 * h, 2 * h + 2)
+            nc.vector.scalar_tensor_tensor(y[:, rows, :], resid[:, rows, :], 0.5, p_ps[h][:], ALU.mult, ALU.add)
+        for h in range(2):
+            rows = slice(2 * h, 2 * h + 2)
+            nc.vector.scalar_tensor_tensor(
+                y[:, rows, 1:O], p_ps[h][:, :, 0 : O - 1], -0.7, y[:, rows, 1:O], ALU.mult, ALU.add
+            )
+        nc.sync.dma_start(out=out_rows, in_=y[:])
+
+        y_bf = sb.tile([P, PACK * O], BF16, name="y_bf", align_bytes=64)
+        nc.vector.tensor_copy(woven(y_bf[:]), by_rows(y[:]))
+        y_codes = sb.tile([P, O], U32, name="y_codes", align_bytes=64)
+        y_plane = sb.tile([P, O], U8, name="y_plane", align_bytes=64)
+        nc.vector.quantize_mx(out=y_codes[:].bitcast(E4M3), scales=y_plane[:], in_=y_bf[:])
+        nc.sync.dma_start(out=out_1[0].rearrange("p c t -> p (c t)").bitcast(I32), in_=y_codes[:].bitcast(I32))
+        for q in range(4):
+            queue = nc.scalar if q % 2 == 0 else nc.sync
+            queue.dma_start(out=out_2[0, 4 * q : 4 * q + 4, :].bitcast(I32), in_=y_plane[32 * q : 32 * q + 4, :].bitcast(I32))

@@ -61,6 +61,9 @@ def tile_list_looks_largerpicks_farther_lagged_pl_kernel(
         resid = sb.tile([P, PACK, O], F32, name="resid")
 
 
+        warm = sb.tile([P, 2], F32, name="warm")
+        nc.vector.memset(warm[:, 0:1], 0.0)
+        nc.scalar.activation(warm[:, 1:2], warm[:, 0:1], ACT.Abs)
         load_scale_rows(nc.gpsimd, wbs_raw, wb_scales)
         x_rows = xf.rearrange("(p t) c -> p t c", t=PACK)
         nc.sync.dma_start(out=x[0][:], in_=x_rows[:, 0, :])

@@ -36,8 +36,10 @@ def load_scale_rows(queue, tile, scales):
         queue.dma_start(out=tile[32 * q : 32 * (q + 1), :].bitcast(I32), in_=rows.unsqueeze(0).broadcast_to([8, 4, rows.shape[1]]))
 
 
-def deal(nc, dealt, raw):
-    nc.vector.tensor_copy(out=dealt.rearrange("p (t m) -> p t m", t=PACK), in_=raw.rearrange("p (m t) -> p t m", t=PACK))
+def deal(nc, dealt, raw, run):
+    nc.vector.tensor_copy(
+        out=dealt.rearrange("p (t b i) -> p b t i", t=PACK, i=run), in_=raw.rearrange("p (b i t) -> p b t i", t=PACK, i=run)
+    )
 
 
 def tile_list_looks_largerpicks_farther_lagged_pl_kernel(
@@ -80,7 +82,7 @@ def tile_list_looks_largerpicks_farther_lagged_pl_kernel(
         nc.sync.dma_start(out=resid[:], in_=rs.rearrange("(p t) o -> p t o", t=PACK))
 
         w_plane = sb.tile([P, R], U8, name="w_plane", align_bytes=64)
-        deal(nc, w_plane[:], ws_raw[:])
+        deal(nc, w_plane[:], ws_raw[:], 16)
         last = PACK - 1
         hj = J // 2
         first = sb.tile([P, PACK, J], F32, name="first")
@@ -115,17 +117,15 @@ def tile_list_looks_largerpicks_farther_lagged_pl_kernel(
                 out=u_codes[:, slots].bitcast(E4M3), scales=u_plane[:, slots], in_=u_bf[:, h * PACK * hj : (h + 1) * PACK * hj]
             )
 
-        w_codes = [sb.tile([P, P], U32, name="w_codes%d" % t, align_bytes=64) for t in range(PACK)]
-        for t in range(PACK):
-            nc.vector.tensor_copy(w_codes[t][:], w_raw[:].rearrange("p (m t) -> p t m", t=PACK)[:, t, :])
+        w_codes = sb.tile([P, R], U32, name="w_codes", align_bytes=64)
+        deal(nc, w_codes[:], w_raw[:], 4)
 
         a_ps = [ps.tile([P, J], F32, name="a_ps%d" % t) for t in range(PACK)]
         for t in range(PACK):
-            for h in range(2):
-                slots = slice(h * hj, (h + 1) * hj)
+            for slots in (slice(0, hj), slice(hj, J)) if t == 0 else (slice(0, J),):
                 nc.tensor.matmul_mx(
                     out=a_ps[t][:, slots],
-                    lhsT=w_codes[t][:].bitcast(E4M3),
+                    lhsT=w_codes[:, t * P : (t + 1) * P].bitcast(E4M3),
                     lhsT_scale=w_plane[:, t * P : (t + 1) * P],
                     rhs=u_codes[:, slots].bitcast(E4M3),
                     rhs_scale=u_plane[:, slots],
@@ -136,15 +136,16 @@ def tile_list_looks_largerpicks_farther_lagged_pl_kernel(
         wb_dealt = sb.tile([P, 3 * N], U8, name="wb_dealt", tag="shared_a", align_bytes=64)
         wb_codes = wb_dealt[:, 0 : 2 * N]
         wb_plane = wb_dealt[:, 2 * N : 3 * N]
-        deal(nc, wb_codes.bitcast(U16), wb_raw[:].bitcast(U16))
-        deal(nc, wb_plane, wbs_raw[:])
+        deal(nc, wb_codes.bitcast(U16), wb_raw[:].bitcast(U16), 8)
+        deal(nc, wb_plane, wbs_raw[:], 16)
 
         a = [sb.tile([P, J], F32, name="a%d" % t) for t in range(PACK)]
         half = sb.tile([P, PACK, O], F32, name="half")
         whole = sb.tile([P, O], F32, name="whole")
         diff = sb.tile([P, PACK, O], F32, name="diff")
-        nc.scalar.copy(a[0][:], a_ps[0][:])
-        for t in range(1, PACK):
+        for t in range(2):
+            nc.scalar.copy(a[t][:], a_ps[t][:])
+        for t in range(2, PACK):
             nc.vector.tensor_copy(a[t][:], a_ps[t][:])
         for t in range(PACK):
             nc.scalar.activation(half[:, t, :], a[t][:].indirect(list4[:]), ACT.Copy, scale=-0.5)

@@ -30,8 +30,8 @@ def by_rows(rows):
     return rows.rearrange("p t (c i) -> p c t i", i=RUN)
 
 
-def load_scale_rows(queue, tile, scales):
-    for q in range(4):
+def load_scale_rows(queue, tile, scales, quadrants):
+    for q in quadrants:
         rows = scales[0, 4 * q : 4 * q + 4, :].bitcast(I32)
         queue.dma_start(out=tile[32 * q : 32 * (q + 1), :].bitcast(I32), in_=rows.unsqueeze(0).broadcast_to([8, 4, rows.shape[1]]))
 
@@ -63,17 +63,18 @@ def tile_list_looks_largerpicks_farther_lagged_pl_kernel(
         resid = sb.tile([P, PACK, O], F32, name="resid")
 
 
+        load_scale_rows(nc.scalar, wbs_raw, wb_scales, (0, 1))
+        load_scale_rows(nc.gpsimd, wbs_raw, wb_scales, (2, 3))
         warm = sb.tile([P, 2], F32, name="warm")
         nc.vector.memset(warm[:, 0:1], 0.0)
         nc.scalar.activation(warm[:, 1:2], warm[:, 0:1], ACT.Abs)
-        load_scale_rows(nc.gpsimd, wbs_raw, wb_scales)
         x_rows = xf.rearrange("(p t) c -> p t c", t=PACK)
         nc.sync.dma_start(out=x[0][:], in_=x_rows[:, 0, :])
         nc.sync.dma_start(list2[:], offs2)
         nc.sync.dma_start(list1[:], offs)
         for t in range(1, PACK):
             nc.sync.dma_start(out=x[t][:], in_=x_rows[:, t, :])
-        load_scale_rows(nc.sync, ws_raw, w_scales)
+        load_scale_rows(nc.sync, ws_raw, w_scales, range(4))
         nc.sync.dma_start(out=factor[:], in_=fk.rearrange("(p t) o -> p (t o)", t=PACK))
         nc.sync.dma_start(out=w_raw[:].bitcast(I32), in_=w_words[0].rearrange("p c t -> p (c t)").bitcast(I32))
         nc.sync.dma_start(out=wb_raw[:].bitcast(I32), in_=wb_words[0].bitcast(I32))
@@ -87,7 +88,7 @@ def tile_list_looks_largerpicks_farther_lagged_pl_kernel(
         hj = J // 2
         first = sb.tile([P, PACK, J], F32, name="first")
         second = sb.tile([P, PACK, J], F32, name="second")
-        larger = [sb.tile([P, PACK, hj], F32, name="larger%d" % h) for h in range(2)]
+        larger = sb.tile([P, 2, PACK, hj], F32, name="larger")
         for t in range(last):
             nc.scalar.activation(second[:, t, :], x[t][:].indirect(list2[:]), ACT.Copy)
             nc.vector.tensor_copy(first[:, t, :], x[t][:].indirect(list1[:]))
@@ -96,10 +97,16 @@ def tile_list_looks_largerpicks_farther_lagged_pl_kernel(
             entries = slice(h * hj // 16, (h + 1) * hj // 16)
             nc.scalar.activation(second[:, last, slots], x[last][:].indirect(list2[:, entries]), ACT.Copy)
             nc.scalar.activation(first[:, last, slots], x[last][:].indirect(list1[:, entries]), ACT.Copy)
-        for planes in (slice(0, last), slice(last, PACK)):
-            for h in range(2):
-                slots = slice(h * hj, (h + 1) * hj)
-                nc.vector.tensor_tensor(larger[h][:, planes, :], first[:, planes, slots], second[:, planes, slots], ALU.max)
+        for planes in (slice(0, 2), slice(2, last)):
+            nc.vector.tensor_tensor(
+                larger[:, :, planes, :],
+                first[:, planes, :].rearrange("p t (h c) -> p h t c", h=2),
+                second[:, planes, :].rearrange("p t (h c) -> p h t c", h=2),
+                ALU.max,
+            )
+        for h in range(2):
+            slots = slice(h * hj, (h + 1) * hj)
+            nc.vector.tensor_tensor(larger[:, h, last, :], first[:, last, slots], second[:, last, slots], ALU.max)
 
         u_bf = sb.tile([P, PACK * J], BF16, name="u_bf", tag="shared_a", align_bytes=64)
         u_codes = sb.tile([P, J], U32, name="u_codes", align_bytes=64)
@@ -107,7 +114,7 @@ def tile_list_looks_largerpicks_farther_lagged_pl_kernel(
         for h in range(2):
             nc.vector.tensor_tensor(
                 woven(u_bf[:, h * PACK * hj : (h + 1) * PACK * hj]),
-                by_rows(larger[h][:]),
+                by_rows(larger[:, h, :, :]),
                 factor[:].unsqueeze(1).unsqueeze(3).to_broadcast([P, hj // RUN, PACK, RUN]),
                 ALU.mult,
             )
@@ -181,18 +188,24 @@ def tile_list_looks_largerpicks_farther_lagged_pl_kernel(
         for h in range(2):
             rows = slice(2 * h, 2 * h + 2)
             nc.vector.scalar_tensor_tensor(y[:, rows, :], resid[:, rows, :], 0.5, p_ps[h][:], ALU.mult, ALU.add)
+        lagged = [slice(1, ho), slice(ho, O)]
         for h in range(2):
             rows = slice(2 * h, 2 * h + 2)
-            nc.vector.scalar_tensor_tensor(
-                y[:, rows, 1:O], p_ps[h][:, :, 0 : O - 1], -0.7, y[:, rows, 1:O], ALU.mult, ALU.add
-            )
+            for part in lagged:
+                before = slice(part.start - 1, part.stop - 1)
+                nc.vector.scalar_tensor_tensor(y[:, rows, part], p_ps[h][:, :, before], -0.7, y[:, rows, part], ALU.mult, ALU.add)
         nc.sync.dma_start(out=out_rows, in_=y[:])
 
         y_bf = sb.tile([P, PACK * O], BF16, name="y_bf", align_bytes=64)
-        nc.vector.tensor_copy(woven(y_bf[:]), by_rows(y[:]))
         y_codes = sb.tile([P, O], U32, name="y_codes", align_bytes=64)
         y_plane = sb.tile([P, O], U8, name="y_plane", align_bytes=64)
-        nc.vector.quantize_mx(out=y_codes[:].bitcast(E4M3), scales=y_plane[:], in_=y_bf[:])
+        for h in range(2):
+            nc.vector.tensor_copy(woven(y_bf[:, h * PACK * ho : (h + 1) * PACK * ho]), by_rows(y[:, :, h * ho : (h + 1) * ho]))
+        for h in range(2):
+            places = slice(h * ho, (h + 1) * ho)
+            nc.vector.quantize_mx(
+                out=y_codes[:, places].bitcast(E4M3), scales=y_plane[:, places], in_=y_bf[:, h * PACK * ho : (h + 1) * PACK * ho]
+            )
         nc.sync.dma_start(out=out_1[0].rearrange("p c t -> p (c t)").bitcast(I32), in_=y_codes[:].bitcast(I32))
         for q in range(4):
             queue = nc.scalar if q % 2 == 0 else nc.sync

from contextlib import ExitStack

import concourse.mybir as mybir

K, T, J, R, O, N = 512, 512, 256, 512, 128, 512
FLOPS = 2 * K * R * J + 2 * R * N * O

F32 = mybir.dt.float32
BF16 = mybir.dt.bfloat16
I32 = mybir.dt.int32
U32 = mybir.dt.uint32
U16 = mybir.dt.uint16
U8 = mybir.dt.uint8
E4M3 = mybir.dt.float8_e4m3fn_x4
E5M2 = mybir.dt.float8_e5m2_x4
E2M1 = mybir.dt.float4_e2m1fn_x4
ALU = mybir.AluOpType
ACT = mybir.ActivationFunctionType

P = 128
PACK = 4
RUN = 4


def woven(cols):
    return cols.rearrange("p (c i t) -> p c t i", i=RUN, t=PACK)


def by_rows(rows):
    return rows.rearrange("p t (c i) -> p c t i", i=RUN)


def load_scale_rows(queue, tile, scales, quadrants):
    for q in quadrants:
        rows = scales[0, 4 * q : 4 * q + 4, :].bitcast(I32)
        queue.dma_start(out=tile[32 * q : 32 * (q + 1), :].bitcast(I32), in_=rows.unsqueeze(0).broadcast_to([8, 4, rows.shape[1]]))


def deal(nc, dealt, raw, run):
    nc.vector.tensor_copy(
        out=dealt.rearrange("p (t b i) -> p b t i", t=PACK, i=run), in_=raw.rearrange("p (b i t) -> p b t i", t=PACK, i=run)
    )


def tile_list_looks_largerpicks_farther_lagged_pl_kernel(
    tc, xf, fk, w_words, w_scales, wb_words, wb_scales, rs, offs, offs2, offs3, offs4, out_0, out_1, out_2
):
    nc = tc.nc
    with ExitStack() as ctx:
        sb = ctx.enter_context(tc.tile_pool(name="sb", bufs=1))
        ps = ctx.enter_context(tc.psum_pool(name="ps", bufs=1))

        list1 = sb.tile([P, J // 16], U16, name="list1")
        list2 = sb.tile([P, J // 16], U16, name="list2")
        list3 = sb.tile([P, O // 16], U16, name="list3")
        list4 = sb.tile([P, O // 16], U16, name="list4")
        x = [sb.tile([P, T], F32, name="x%d" % t) for t in range(PACK)]
        factor = sb.tile([P, PACK], F32, name="factor")
        w_raw = sb.tile([P, R], U32, name="w_raw")
        ws_raw = sb.tile([P, R], U8, name="ws_raw")
        wb_raw = sb.tile([P, 2 * N], U8, name="wb_raw")
        wbs_raw = sb.tile([P, N], U8, name="wbs_raw")
        resid = sb.tile([P, PACK, O], F32, name="resid")


        load_scale_rows(nc.scalar, wbs_raw, wb_scales, (0, 1))
        load_scale_rows(nc.gpsimd, wbs_raw, wb_scales, (2, 3))
        warm = sb.tile([P, 2], F32, name="warm")
        nc.vector.memset(warm[:, 0:1], 0.0)
        nc.scalar.activation(warm[:, 1:2], warm[:, 0:1], ACT.Abs)
        x_rows = xf.rearrange("(p t) c -> p t c", t=PACK)
        nc.sync.dma_start(out=x[0][:], in_=x_rows[:, 0, :])
        nc.sync.dma_start(list2[:], offs2)
        nc.sync.dma_start(list1[:], offs)
        for t in range(1, PACK):
            nc.sync.dma_start(out=x[t][:], in_=x_rows[:, t, :])
        load_scale_rows(nc.sync, ws_raw, w_scales, range(4))
        nc.sync.dma_start(out=factor[:], in_=fk.rearrange("(p t) o -> p (t o)", t=PACK))
        nc.sync.dma_start(out=w_raw[:].bitcast(I32), in_=w_words[0].rearrange("p c t -> p (c t)").bitcast(I32))
        nc.sync.dma_start(out=wb_raw[:].bitcast(I32), in_=wb_words[0].bitcast(I32))
        nc.sync.dma_start(list4[:], offs4)
        nc.sync.dma_start(list3[:], offs3)
        nc.sync.dma_start(out=resid[:], in_=rs.rearrange("(p t) o -> p t o", t=PACK))

        w_plane = sb.tile([P, R], U8, name="w_plane", align_bytes=64)
        deal(nc, w_plane[:], ws_raw[:], 16)
        last = PACK - 1
        hj = J // 2
        first = sb.tile([P, PACK, J], F32, name="first")
        second = sb.tile([P, PACK, J], F32, name="second")
        larger = sb.tile([P, 2, PACK, hj], F32, name="larger")
        for t in range(last):
            nc.scalar.activation(second[:, t, :], x[t][:].indirect(list2[:]), ACT.Copy)
            nc.vector.tensor_copy(first[:, t, :], x[t][:].indirect(list1[:]))
        for h in range(2):
            slots = slice(h * hj, (h + 1) * hj)
            entries = slice(h * hj // 16, (h + 1) * hj // 16)
            nc.scalar.activation(second[:, last, slots], x[last][:].indirect(list2[:, entries]), ACT.Copy)
            nc.scalar.activation(first[:, last, slots], x[last][:].indirect(list1[:, entries]), ACT.Copy)
        for planes in (slice(0, 2), slice(2, last)):
            nc.vector.tensor_tensor(
                larger[:, :, planes, :],
                first[:, planes, :].rearrange("p t (h c) -> p h t c", h=2),
                second[:, planes, :].rearrange("p t (h c) -> p h t c", h=2),
                ALU.max,
            )
        for h in range(2):
            slots = slice(h * hj, (h + 1) * hj)
            nc.vector.tensor_tensor(larger[:, h, last, :], first[:, last, slots], second[:, last, slots], ALU.max)

        u_bf = sb.tile([P, PACK * J], BF16, name="u_bf", tag="shared_a", align_bytes=64)
        u_codes = sb.tile([P, J], U32, name="u_codes", align_bytes=64)
        u_plane = sb.tile([P, J], U8, name="u_plane", align_bytes=64)
        for h in range(2):
            nc.vector.tensor_tensor(
                woven(u_bf[:, h * PACK * hj : (h + 1) * PACK * hj]),
                by_rows(larger[:, h, :, :]),
                factor[:].unsqueeze(1).unsqueeze(3).to_broadcast([P, hj // RUN, PACK, RUN]),
                ALU.mult,
            )
        for h in range(2):
            slots = slice(h * hj, (h + 1) * hj)
            nc.vector.quantize_mx(
                out=u_codes[:, slots].bitcast(E4M3), scales=u_plane[:, slots], in_=u_bf[:, h * PACK * hj : (h + 1) * PACK * hj]
            )

        w_codes = sb.tile([P, R], U32, name="w_codes", align_bytes=64)
        deal(nc, w_codes[:], w_raw[:], 4)

        a_ps = [ps.tile([P, J], F32, name="a_ps%d" % t) for t in range(PACK)]
        for t in range(PACK):
            for slots in (slice(0, hj), slice(hj, J)) if t == 0 else (slice(0, J),):
                nc.tensor.matmul_mx(
                    out=a_ps[t][:, slots],
                    lhsT=w_codes[:, t * P : (t + 1) * P].bitcast(E4M3),
                    lhsT_scale=w_plane[:, t * P : (t + 1) * P],
                    rhs=u_codes[:, slots].bitcast(E4M3),
                    rhs_scale=u_plane[:, slots],
                    start=True,
                    stop=True,
                )

        wb_dealt = sb.tile([P, 3 * N], U8, name="wb_dealt", tag="shared_a", align_bytes=64)
        wb_codes = wb_dealt[:, 0 : 2 * N]
        wb_plane = wb_dealt[:, 2 * N : 3 * N]
        deal(nc, wb_codes.bitcast(U16), wb_raw[:].bitcast(U16), 8)
        deal(nc, wb_plane, wbs_raw[:], 16)

        a = [sb.tile([P, J], F32, name="a%d" % t) for t in range(PACK)]
        half = sb.tile([P, PACK, O], F32, name="half")
        whole = sb.tile([P, O], F32, name="whole")
        diff = sb.tile([P, PACK, O], F32, name="diff")
        for t in range(2):
            nc.scalar.copy(a[t][:], a_ps[t][:])
        for t in range(2, PACK):
            nc.vector.tensor_copy(a[t][:], a_ps[t][:])
        for t in range(PACK):
            nc.scalar.activation(half[:, t, :], a[t][:].indirect(list4[:]), ACT.Copy, scale=-0.5)
        nc.scalar.activation(whole[:], a[last][:].indirect(list3[:]), ACT.Copy)
        for t in range(last):
            nc.vector.tensor_tensor(diff[:, t, :], a[t][:].indirect(list3[:]), half[:, t, :], ALU.add)
        nc.vector.tensor_tensor(diff[:, last, :], whole[:], half[:, last, :], ALU.add)

        hid_bf = sb.tile([P, PACK * O], BF16, name="hid_bf", align_bytes=64)
        ho = O // 2
        nc.scalar.activation(woven(hid_bf[:, 0 : PACK * ho]), by_rows(diff[:, :, 0:ho]), ACT.Abs)
        upper = diff[:, :, ho:O].rearrange("p t c -> p c t")
        nc.vector.scalar_tensor_tensor(
            hid_bf[:, PACK * ho : PACK * O].rearrange("p (c t) -> p c t", t=PACK), upper, -1.0, upper, ALU.mult, ALU.max
        )
        hid_codes = sb.tile([P, O], U32, name="hid_codes", align_bytes=64)
        hid_plane = sb.tile([P, O], U8, name="hid_plane", align_bytes=64)
        nc.vector.quantize_mx(out=hid_codes[:].bitcast(E5M2), scales=hid_plane[:], in_=hid_bf[:])

        p_ps = [ps.tile([P, 2, O], F32, name="p_ps%d" % h) for h in range(2)]
        y = sb.tile([P, PACK, O], F32, name="y")
        out_rows = out_0.rearrange("(p t) o -> p t o", t=PACK)
        for t in range(PACK):
            nc.tensor.matmul_mx(
                out=p_ps[t // 2][:, t % 2, :],
                lhsT=wb_codes[:, 2 * t * P : 2 * (t + 1) * P].bitcast(E2M1),
                lhsT_scale=wb_plane[:, t * P : (t + 1) * P],
                rhs=hid_codes[:].bitcast(E5M2),
                rhs_scale=hid_plane[:],
                start=True,
                stop=True,
            )
        for h in range(2):
            rows = slice(2 * h, 2 * h + 2)
            nc.vector.scalar_tensor_tensor(y[:, rows, :], resid[:, rows, :], 0.5, p_ps[h][:], ALU.mult, ALU.add)
        lagged = [slice(1, ho), slice(ho, O)]
        for h in range(2):
            rows = slice(2 * h, 2 * h + 2)
            for part in lagged:
                before = slice(part.start - 1, part.stop - 1)
                nc.vector.scalar_tensor_tensor(y[:, rows, part], p_ps[h][:, :, before], -0.7, y[:, rows, part], ALU.mult, ALU.add)
        nc.sync.dma_start(out=out_rows, in_=y[:])

        y_bf = sb.tile([P, PACK * O], BF16, name="y_bf", align_bytes=64)
        y_codes = sb.tile([P, O], U32, name="y_codes", align_bytes=64)
        y_plane = sb.tile([P, O], U8, name="y_plane", align_bytes=64)
        for h in range(2):
            nc.vector.tensor_copy(woven(y_bf[:, h * PACK * ho : (h + 1) * PACK * ho]), by_rows(y[:, :, h * ho : (h + 1) * ho]))
        for h in range(2):
            places = slice(h * ho, (h + 1) * ho)
            nc.vector.quantize_mx(
                out=y_codes[:, places].bitcast(E4M3), scales=y_plane[:, places], in_=y_bf[:, h * PACK * ho : (h + 1) * PACK * ho]
            )
        nc.sync.dma_start(out=out_1[0].rearrange("p c t -> p (c t)").bitcast(I32), in_=y_codes[:].bitcast(I32))
        for q in range(4):
            queue = nc.scalar if q % 2 == 0 else nc.sync
            queue.dma_start(out=out_2[0, 4 * q : 4 * q + 4, :].bitcast(I32), in_=y_plane[32 * q : 32 * q + 4, :].bitcast(I32))
